import numpy as np
import ml_dtypes


def mxq(x, axis, fmt="e4m3"):
    dtype, down = {"e4m3": (ml_dtypes.float8_e4m3fn, 7), "e5m2": (ml_dtypes.float8_e5m2, 14)}[fmt]
    v = np.moveaxis(np.asarray(x, np.float32).astype(ml_dtypes.bfloat16).astype(np.float64), axis, -1)
    blocks = v.reshape(v.shape[:-1] + (-1, 32))
    amax = np.abs(blocks).max(-1, keepdims=True)
    byte = np.maximum(np.where(amax > 0, np.frexp(amax)[1] - 1 + 127, 0) - down, 1)
    scale = np.exp2(byte - 127.0)
    codes = (blocks / scale).astype(np.float32).astype(dtype).astype(np.float64)
    return np.moveaxis((codes * scale).reshape(v.shape), -1, axis)


WIDE = False


def mx_kscale(k):
    if not WIDE:
        return np.ones(k)
    levels = np.array([10, -10, 5, -5, 0])
    if k % 512:
        return np.exp2(np.random.permutation(np.resize(levels, k // 32))).repeat(32)
    a = np.empty((k // 512, 16))
    for p in range(k // 512):
        a[p, :8] = np.random.permutation(np.resize(levels, 8))
        for g in range(8):
            far = levels[np.abs(levels - a[p, g]) >= 10]
            a[p, g + 8] = far[np.random.randint(len(far))]
    return np.exp2(a.ravel()).repeat(32)


BF16 = ml_dtypes.bfloat16


def bf(x):
    return np.asarray(x, np.float32).astype(BF16)


def f64(x):
    return np.asarray(x).astype(np.float64)


E2M1 = np.array([0.0, 0.5, 1.0, 1.5, 2.0, 3.0, 4.0, 6.0, -0.0, -0.5, -1.0, -1.5, -2.0, -3.0, -4.0, -6.0])


def pack_weight(w, fmt):
    k, n = w.shape
    w = f64(bf(w)).reshape(k // 32, 32, n)
    amax = np.abs(w).max(1)
    if fmt == "e4m3":
        byte = np.frexp(amax)[1] - 1 + 127 - 7
    else:
        mant, ex = np.frexp(amax / 6.0)
        byte = np.where(mant > 0.5, ex, ex - 1) + 127
    byte = np.clip(np.where(amax > 0, byte, 1), 1, 254)
    scaled = (w * np.exp2(127.0 - byte)[:, None, :]).reshape(k, n).astype(np.float32)
    by_word = np.ascontiguousarray(scaled.reshape(k // 512, 128, 4, n).transpose(0, 1, 3, 2))
    if fmt == "e4m3":
        words = by_word.astype(ml_dtypes.float8_e4m3fn).view(np.uint8)
    else:
        c = by_word.astype(ml_dtypes.float4_e2m1fn).view(np.uint8) & 0xF
        words = c[..., 0::2] | (c[..., 1::2] << 4)
    return np.ascontiguousarray(words), np.ascontiguousarray(byte.astype(np.uint8).reshape(k // 512, 16, n))


def unpack_weight(words, scales, fmt):
    g, p, n, _ = words.shape
    if fmt == "e4m3":
        vals = np.ascontiguousarray(words).view(ml_dtypes.float8_e4m3fn).astype(np.float64)
    else:
        nib = np.empty((g, p, n, 4), np.uint8)
        nib[..., 0::2] = words & 0xF
        nib[..., 1::2] = words >> 4
        vals = E2M1[nib]
    vals = vals * np.repeat(np.exp2(scales.astype(np.float64) - 127.0), 8, axis=1)[..., None]
    return vals.transpose(0, 1, 3, 2).reshape(g * 512, n)
def pack4(w):
    words, scales = pack_weight(w, "e2m1")
    return words.reshape(words.shape[0], 128, -1), scales


def unpack4(words, scales):
    return unpack_weight(words.reshape(words.shape[0], 128, -1, 2), scales, "e2m1")


M, D, N = 1024, 1536, 1024


def setup_inputs():
    s = mx_kscale(D)
    start = np.random.standard_normal((M, D))
    end = np.random.standard_normal((M, D))
    gate_w = np.random.standard_normal((D, N)) / np.sqrt(D) / s[:, None]
    value_w = np.random.standard_normal((D, N)) / np.sqrt(D) / s[:, None]
    w1_words, w1_scales = pack4(gate_w)
    w2_words, w2_scales = pack_weight(value_w, "e4m3")
    return {"noise": bf(start * s),
            "delta": bf((end - start) * s),
            "tau": bf(0.05 + 0.9 * np.random.random((M, 1))),
            "w1_words": w1_words, "w1_scales": w1_scales,
            "w2_words": w2_words, "w2_scales": w2_scales,
            "w3": bf(np.random.standard_normal((D, N)) / np.sqrt(D) / s[:, None]),
            "target": bf(np.random.standard_normal((M, N)))}


def reference(noise, delta, tau, w1_words, w1_scales, w2_words, w2_scales, w3, target):
    z = f64(noise) + f64(tau) * f64(delta)
    zq = mxq(z, 1, "e4m3")
    a = zq @ unpack4(w1_words, w1_scales)
    b = zq @ unpack_weight(w2_words, w2_scales, "e4m3")
    c = zq @ mxq(f64(w3), 0, "e4m3")
    velocity = np.tanh(a) * b + c
    return velocity - f64(target)

@@ -1,0 +1,314 @@
+from contextlib import ExitStack
+
+import concourse.mybir as mybir
+from concourse.masks import make_identity
+
+M, D, N = 1024, 1536, 1024
+FLOPS = 3 * 2 * M * D * N
+
+F32 = mybir.dt.float32
+BF16 = mybir.dt.bfloat16
+I32 = mybir.dt.int32
+U32 = mybir.dt.uint32
+U8 = mybir.dt.uint8
+FP8X4 = mybir.dt.float8_e4m3fn_x4
+FP4X4 = mybir.dt.float4_e2m1fn_x4
+ALU = mybir.AluOpType
+ACT = mybir.ActivationFunctionType
+
+P = 128
+PACK = 4
+PASSES = D // (P * PACK)
+TILES = M // P
+HALF = 512
+HALVES = N // HALF
+MX_BANKS = 6
+W2_ROW = 4
+PIECE = 128
+FIRST_W3_STEP = 3
+PIECES_PER_STEP = 3
+ORDER = [("z",4),("z",5),("w",0),("z",6),("w",1),("t",0),("z",7),("w",2),("t",1),("t",2),("t",3)]
+V_TAIL = 0
+
+
+def tile_straight_path_regression_error_s10_kernel(
+    tc, noise, delta, tau, w1_words, w1_scales, w2_words, w2_scales, w3, target, out
+):
+    nc = tc.nc
+    noise_t = noise.rearrange("(p t) k -> t p k", t=TILES)
+    delta_t = delta.rearrange("(p t) k -> t p k", t=TILES)
+    target_p = target.rearrange("(p t) n -> p t n", t=TILES)
+    out_t = out.rearrange("(p t) n -> t p n", t=TILES)
+
+    with ExitStack() as ctx:
+        keep = ctx.enter_context(tc.tile_pool(name="keep", bufs=1))
+        ring = ctx.enter_context(tc.tile_pool(name="ring", bufs=3))
+        psum = ctx.enter_context(tc.psum_pool(name="psum", bufs=1))
+        ctx.enter_context(tc.manual_schedule())
+
+        w1_planes = keep.tile([P, PASSES, N], U8, name="w1_planes", align_bytes=64)
+        w2_planes = keep.tile([P, PASSES, N], U8, name="w2_planes", align_bytes=64)
+        nc.vector.memset(w1_planes[:].bitcast(I32), 0)
+        nc.vector.memset(w2_planes[:].bitcast(I32), 0)
+        zero = keep.tile([P, 1], F32, name="zero")
+        nc.vector.memset(zero[:], 0.0)
+        no_bias = keep.tile([P, 1], F32, name="no_bias")
+        nc.scalar.activation(out=no_bias[:], in_=zero[:], func=ACT.Tanh)
+        ident = keep.tile([P, P], F32, name="ident")
+        make_identity(nc, ident[:])
+
+        tau_sb = keep.tile([P, TILES], BF16, name="tau_sb")
+        noise_sb, delta_sb, w1_sb, w2_sb, w3_sb, target_sb = {}, {}, {}, {}, {}, {}
+
+        def load_state(t):
+            noise_sb[t] = keep.tile([P, D], BF16, name="noise%d" % t)
+            delta_sb[t] = keep.tile([P, D], BF16, name="delta%d" % t)
+            nc.sync.dma_start(out=noise_sb[t][:], in_=noise_t[t])
+            nc.sync.dma_start(out=delta_sb[t][:], in_=delta_t[t])
+
+        def load_scales(planes, scales, row):
+            rows = scales.rearrange("g (q r) n -> r q g n", r=4)
+            for r in range(4):
+                nc.sync.dma_start(
+                    out=planes[row + r : P : 32, :, :].bitcast(I32), in_=rows[r].bitcast(I32)
+                )
+
+        def load_w1(h):
+            w1_sb[h] = keep.tile([P, PASSES, 2 * HALF], U8, name="w1_%d" % h, align_bytes=64)
+            src = w1_words.rearrange("g p b -> p g b")[:, :, 2 * HALF * h : 2 * HALF * (h + 1)]
+            nc.sync.dma_start(out=w1_sb[h][:].bitcast(I32), in_=src.bitcast(I32))
+
+        def load_w2(h):
+            w2_sb[h] = keep.tile([P, PASSES, HALF], U32, name="w2_%d" % h, align_bytes=64)
+            src = w2_words.rearrange("g p n t -> p g (n t)")[:, :, PACK * HALF * h : PACK * HALF * (h + 1)]
+            nc.sync.dma_start(out=w2_sb[h][:].bitcast(I32), in_=src.bitcast(I32))
+
+        def load_w3(g):
+            w3_sb[g] = keep.tile([P, PACK, N], BF16, name="w3_%d" % g)
+            rows = w3[P * PACK * g : P * PACK * (g + 1), :]
+            nc.sync.dma_start(out=w3_sb[g][:], in_=rows.rearrange("(p j) n -> p j n", j=PACK))
+
+        def load_target(pair):
+            target_sb[pair] = keep.tile([P, 2, N], BF16, name="target%d" % pair)
+            nc.sync.dma_start(out=target_sb[pair][:], in_=target_p[:, 2 * pair : 2 * pair + 2, :])
+
+        nc.sync.dma_start(out=tau_sb[:], in_=tau.rearrange("(p t) o -> p (t o)", t=TILES))
+        load_state(0)
+        load_state(1)
+        load_scales(w1_planes, w1_scales, 0)
+        load_w1(0)
+        load_w1(1)
+        load_state(2)
+        load_scales(w2_planes, w2_scales, W2_ROW)
+        load_w2(0)
+        load_state(3)
+        load_w2(1)
+        for kind, i in ORDER:
+            {"z": load_state, "w": load_w3, "t": load_target}[kind](i)
+
+        z_sorted, z_grouped, z_codes, z_scales = {}, {}, {}, {}
+        w3_grouped, w3_codes, w3_scales = {}, {}, {}
+        sums, acc = {}, {}
+        opened = []
+
+        groups = ((0, 2), (2, 1))
+
+        def interpolate(t, group, u):
+            first, count = groups[group]
+            cols = slice(P * PACK * first, P * PACK * (first + count))
+            z_sorted[t, group, u] = ring.tile([P, count * P * 2], BF16, name="z_sorted%d_%d" % (group, u))
+            nc.vector.scalar_tensor_tensor(
+                out=z_sorted[t, group, u][:].rearrange("p (q e) -> p q e", e=2),
+                in0=delta_sb[t][:, cols].rearrange("p (q u e) -> p u q e", u=2, e=2)[:, u],
+                scalar=tau_sb[:, t : t + 1],
+                in1=noise_sb[t][:, cols].rearrange("p (q u e) -> p u q e", u=2, e=2)[:, u],
+                op0=ALU.mult,
+                op1=ALU.add,
+            )
+
+        def interpolate_tile(t):
+            for group in range(2):
+                for u in range(2):
+                    interpolate(t, group, u)
+
+        def turn(t, group):
+            first, count = groups[group]
+            bank = psum.tile([P, 2, count, P], F32, name="turn%d" % group)
+            for u in range(2):
+                words = z_sorted[t, group, u][:].bitcast(F32)
+                for i in range(count):
+                    nc.tensor.transpose(bank[:, u, i, :], words[:, P * i : P * (i + 1)], ident[:])
+            z_grouped[t, group] = ring.tile(
+                [P, count * P * PACK], BF16, name="z_grouped%d" % group, align_bytes=64
+            )
+            nc.scalar.copy(
+                out=z_grouped[t, group][:].bitcast(F32).rearrange("p (c u) -> p c u", u=2),
+                in_=bank[:].rearrange("p u i m -> p (i m) u"),
+            )
+
+        def turn_tile(t):
+            turn(t, 0)
+            turn(t, 1)
+
+        def quantize_state(t, group):
+            first, count = groups[group]
+            codes = keep.tile([P, count * P], U32, name="z_codes%d_%d" % (t, group), align_bytes=64)
+            scales = keep.tile([P, count * P], U8, name="z_scales%d_%d" % (t, group), align_bytes=64)
+            nc.vector.quantize_mx(out=codes[:].bitcast(FP8X4), scales=scales[:], in_=z_grouped[t, group][:])
+            for i in range(count):
+                z_codes[t, first + i] = codes[:, P * i : P * (i + 1)]
+                z_scales[t, first + i] = scales[:, P * i : P * (i + 1)]
+
+        def quantize_tile(t):
+            quantize_state(t, 0)
+            quantize_state(t, 1)
+
+        def product(kind, t, h):
+            bank = psum.tile([P, HALF], F32, name="mx%d" % (len(opened) % MX_BANKS))
+            opened.append(kind)
+            sums[kind, t, h] = bank
+            cols = slice(HALF * h, HALF * (h + 1))
+            for g in range(PASSES):
+                if kind == 1:
+                    rhs, rhs_scale = w1_sb[h][:, g, :].bitcast(FP4X4), w1_planes[:, g, cols]
+                elif kind == 2:
+                    rhs, rhs_scale = w2_sb[h][:, g, :].bitcast(FP8X4), w2_planes[W2_ROW:P, g, cols]
+                else:
+                    rhs, rhs_scale = w3_codes[g, h][:].bitcast(FP8X4), w3_scales[g, h][:]
+                nc.tensor.matmul_mx(
+                    out=bank[:],
+                    lhsT=z_codes[t, g].bitcast(FP8X4),
+                    lhsT_scale=z_scales[t, g],
+                    rhs=rhs,
+                    rhs_scale=rhs_scale,
+                    start=(g == 0),
+                    stop=(g == PASSES - 1),
+                )
+
+        def gate(t, h):
+            acc[t, h] = keep.tile([P, HALF], F32, name="acc%d_%d" % (t, h))
+            nc.scalar.activation(out=acc[t, h][:], in_=sums[1, t, h][:], func=ACT.Tanh, bias=no_bias[:])
+
+        def apply_gate(t, h):
+            nc.vector.tensor_tensor(out=acc[t, h][:], in0=sums[2, t, h][:], in1=acc[t, h][:], op=ALU.mult)
+
+        def subtract_target(t, h):
+            engine = nc.vector if h == 1 and t >= TILES - V_TAIL else nc.gpsimd
+            engine.tensor_tensor(
+                out=acc[t, h][:],
+                in0=acc[t, h][:],
+                in1=target_sb[t // 2][:, t % 2, HALF * h : HALF * (h + 1)],
+                op=ALU.subtract,
+            )
+
+        def finish(t, h):
+            nc.vector.tensor_tensor(out=acc[t, h][:], in0=sums[3, t, h][:], in1=acc[t, h][:], op=ALU.add)
+            nc.sync.dma_start(out=out_t[t][:, HALF * h : HALF * (h + 1)], in_=acc[t, h][:])
+
+        per_block = HALF // PIECE
+        to_group = [(g, h, i) for h in range(HALVES) for g in range(PASSES) for i in range(per_block)]
+        to_quantize = []
+
+        def group_w3():
+            g, h, i = to_group.pop(0)
+            if i == 0:
+                w3_grouped[g, h] = ring.tile([P, HALF, PACK], BF16, name="w3_grouped", align_bytes=64)
+            c0 = HALF * h + PIECE * i
+            nc.scalar.copy(
+                out=w3_grouped[g, h][:, PIECE * i : PIECE * (i + 1), :].rearrange("p (c i) j -> p c j i", i=4),
+                in_=w3_sb[g][:, :, c0 : c0 + PIECE].rearrange("p j (c i) -> p c j i", i=4),
+            )
+            if i == per_block - 1:
+                to_quantize.append((g, h))
+
+        def quantize_w3():
+            for g, h in list(to_quantize):
+                w3_codes[g, h] = keep.tile([P, HALF], U32, name="w3_codes%d_%d" % (g, h), align_bytes=64)
+                w3_scales[g, h] = keep.tile([P, HALF], U8, name="w3_scales%d_%d" % (g, h), align_bytes=64)
+                nc.vector.quantize_mx(
+                    out=w3_codes[g, h][:].bitcast(FP8X4),
+                    scales=w3_scales[g, h][:],
+                    in_=w3_grouped[g, h][:].rearrange("p c j -> p (c j)"),
+                )
+            to_quantize.clear()
+
+        interpolate_tile(0)
+        turn_tile(0)
+        interpolate(1, 0, 0)
+        quantize_state(0, 0)
+        interpolate(1, 0, 1)
+        quantize_state(0, 1)
+        interpolate(1, 1, 0)
+        interpolate(1, 1, 1)
+        product(1, 0, 0)
+        turn_tile(1)
+        product(1, 0, 1)
+        quantize_tile(1)
+        gate(0, 0)
+        gate(0, 1)
+        interpolate_tile(2)
+        product(1, 1, 0)
+        product(1, 1, 1)
+        gate(1, 0)
+        turn_tile(2)
+        gate(1, 1)
+        product(2, 0, 0)
+        product(2, 1, 0)
+        quantize_tile(2)
+        apply_gate(0, 0)
+        interpolate_tile(3)
+        apply_gate(1, 0)
+        product(1, 2, 0)
+        product(1, 2, 1)
+        gate(2, 0)
+        turn_tile(3)
+        gate(2, 1)
+        product(2, 2, 0)
+        product(2, 0, 1)
+        product(2, 1, 1)
+        quantize_tile(3)
+        interpolate_tile(4)
+        apply_gate(2, 0)
+        apply_gate(0, 1)
+
+        late = (1, 1)
+        for s in range(3, TILES + 1):
+            if s + 1 < TILES:
+                turn_tile(s + 1)
+            if s < TILES:
+                product(1, s, 0)
+                product(1, s, 1)
+            apply_gate(*late)
+            if s + 1 < TILES:
+                quantize_tile(s + 1)
+            if s < TILES:
+                gate(s, 0)
+                gate(s, 1)
+            if s + 2 < TILES:
+                interpolate_tile(s + 2)
+            quantize_w3()
+            if s > 3:
+                product(2, s - 1, 0)
+            product(2, s - 1, 1)
+            if s >= FIRST_W3_STEP:
+                for i in range(PIECES_PER_STEP):
+                    group_w3()
+            if s > 3:
+                apply_gate(s - 1, 0)
+            late = (s - 1, 1)
+        apply_gate(*late)
+        while (PASSES - 1, 0) not in w3_grouped or to_group[0][1] == 0:
+            group_w3()
+        quantize_w3()
+
+        for t in range(TILES):
+            subtract_target(t, 0)
+        for h in range(HALVES):
+            for t in range(TILES):
+                product(3, t, h)
+                if h == 1:
+                    subtract_target(t, h)
+                finish(t, h)
+                quantize_w3()
+                for i in range(min(2, len(to_group))):
+                    group_w3()

@@ -18,17 +18,20 @@ ACT = mybir.ActivationFunctionType
 
 P = 128
 PACK = 4
-PASSES = D // (P * PACK)
+K_PASS = P * PACK
+PASSES = D // K_PASS
 TILES = M // P
 HALF = 512
 HALVES = N // HALF
+GROUPS = (range(0, 2), range(2, 3))
 MX_BANKS = 6
-W2_ROW = 4
+W2_SCALE_ROW = 4
+EARLY_TILES = 3
 PIECE = 128
-FIRST_W3_STEP = 3
 PIECES_PER_STEP = 3
-ORDER = [("z",4),("z",5),("w",0),("z",6),("w",1),("t",0),("z",7),("w",2),("t",1),("t",2),("t",3)]
-V_TAIL = 0
+FIRST_W3_STEP = 4
+VECTOR_UNITS = 3
+SECOND_HALF_LAG = 3
 
 
 def tile_straight_path_regression_error_s10_kernel(
@@ -46,183 +49,189 @@ def tile_straight_path_regression_error_s10_kernel(
         psum = ctx.enter_context(tc.psum_pool(name="psum", bufs=1))
         ctx.enter_context(tc.manual_schedule())
 
-        w1_planes = keep.tile([P, PASSES, N], U8, name="w1_planes", align_bytes=64)
-        w2_planes = keep.tile([P, PASSES, N], U8, name="w2_planes", align_bytes=64)
-        nc.vector.memset(w1_planes[:].bitcast(I32), 0)
-        nc.vector.memset(w2_planes[:].bitcast(I32), 0)
+        w1_scale_sb = keep.tile([P, PASSES, N], U8, name="w1_scale_sb", align_bytes=64)
+        w2_scale_sb = keep.tile([P, PASSES, N], U8, name="w2_scale_sb", align_bytes=64)
+        nc.vector.memset(w1_scale_sb[:].bitcast(I32), 0)
+        nc.vector.memset(w2_scale_sb[:].bitcast(I32), 0)
         zero = keep.tile([P, 1], F32, name="zero")
         nc.vector.memset(zero[:], 0.0)
-        no_bias = keep.tile([P, 1], F32, name="no_bias")
-        nc.scalar.activation(out=no_bias[:], in_=zero[:], func=ACT.Tanh)
-        ident = keep.tile([P, P], F32, name="ident")
-        make_identity(nc, ident[:])
+        zero_bias = keep.tile([P, 1], F32, name="zero_bias")
+        nc.scalar.activation(out=zero_bias[:], in_=zero[:], func=ACT.Tanh)
+        identity = keep.tile([P, P], F32, name="identity")
+        make_identity(nc, identity[:])
 
         tau_sb = keep.tile([P, TILES], BF16, name="tau_sb")
-        noise_sb, delta_sb, w1_sb, w2_sb, w3_sb, target_sb = {}, {}, {}, {}, {}, {}
+        state_sb, w1_sb, w2_sb, w3_sb, target_sb = {}, {}, {}, {}, {}
 
-        def load_state(t):
-            noise_sb[t] = keep.tile([P, D], BF16, name="noise%d" % t)
-            delta_sb[t] = keep.tile([P, D], BF16, name="delta%d" % t)
-            nc.sync.dma_start(out=noise_sb[t][:], in_=noise_t[t])
-            nc.sync.dma_start(out=delta_sb[t][:], in_=delta_t[t])
+        def load_state(t, passes):
+            cols = slice(K_PASS * passes.start, K_PASS * passes.stop)
+            width = K_PASS * len(passes)
+            noise_sb = keep.tile([P, width], BF16, name="noise%d_%d" % (t, passes.start))
+            delta_sb = keep.tile([P, width], BF16, name="delta%d_%d" % (t, passes.start))
+            nc.sync.dma_start(out=noise_sb[:], in_=noise_t[t][:, cols])
+            nc.sync.dma_start(out=delta_sb[:], in_=delta_t[t][:, cols])
+            state_sb[t, passes.start] = (noise_sb, delta_sb)
 
-        def load_scales(planes, scales, row):
-            rows = scales.rearrange("g (q r) n -> r q g n", r=4)
+        def load_scales(scale_sb, scales, first_row):
+            rows = scales.rearrange("g (Q r) n -> r Q g n", r=4)
             for r in range(4):
-                nc.sync.dma_start(
-                    out=planes[row + r : P : 32, :, :].bitcast(I32), in_=rows[r].bitcast(I32)
-                )
+                nc.sync.dma_start(out=scale_sb[first_row + r : P : 32, :, :].bitcast(I32), in_=rows[r].bitcast(I32))
 
         def load_w1(h):
             w1_sb[h] = keep.tile([P, PASSES, 2 * HALF], U8, name="w1_%d" % h, align_bytes=64)
-            src = w1_words.rearrange("g p b -> p g b")[:, :, 2 * HALF * h : 2 * HALF * (h + 1)]
-            nc.sync.dma_start(out=w1_sb[h][:].bitcast(I32), in_=src.bitcast(I32))
+            words = w1_words.rearrange("g p b -> p g b")[:, :, 2 * HALF * h : 2 * HALF * (h + 1)]
+            nc.sync.dma_start(out=w1_sb[h][:].bitcast(I32), in_=words.bitcast(I32))
 
         def load_w2(h):
             w2_sb[h] = keep.tile([P, PASSES, HALF], U32, name="w2_%d" % h, align_bytes=64)
-            src = w2_words.rearrange("g p n t -> p g (n t)")[:, :, PACK * HALF * h : PACK * HALF * (h + 1)]
-            nc.sync.dma_start(out=w2_sb[h][:].bitcast(I32), in_=src.bitcast(I32))
+            words = w2_words.rearrange("g p n j -> p g (n j)")[:, :, PACK * HALF * h : PACK * HALF * (h + 1)]
+            nc.sync.dma_start(out=w2_sb[h][:].bitcast(I32), in_=words.bitcast(I32))
 
         def load_w3(g):
             w3_sb[g] = keep.tile([P, PACK, N], BF16, name="w3_%d" % g)
-            rows = w3[P * PACK * g : P * PACK * (g + 1), :]
+            rows = w3[K_PASS * g : K_PASS * (g + 1), :]
             nc.sync.dma_start(out=w3_sb[g][:], in_=rows.rearrange("(p j) n -> p j n", j=PACK))
 
-        def load_target(pair):
-            target_sb[pair] = keep.tile([P, 2, N], BF16, name="target%d" % pair)
-            nc.sync.dma_start(out=target_sb[pair][:], in_=target_p[:, 2 * pair : 2 * pair + 2, :])
+        def load_target(tiles):
+            rows = keep.tile([P, len(tiles), N], BF16, name="target%d" % tiles.start)
+            nc.sync.dma_start(out=rows[:], in_=target_p[:, tiles.start : tiles.stop, :])
+            for t in tiles:
+                target_sb[t] = rows[:, t - tiles.start, :]
 
+        whole = range(PASSES)
         nc.sync.dma_start(out=tau_sb[:], in_=tau.rearrange("(p t) o -> p (t o)", t=TILES))
-        load_state(0)
-        load_state(1)
-        load_scales(w1_planes, w1_scales, 0)
+        load_state(0, GROUPS[0])
+        load_state(0, GROUPS[1])
+        load_state(1, GROUPS[0])
+        load_scales(w1_scale_sb, w1_scales, 0)
         load_w1(0)
+        load_state(1, GROUPS[1])
         load_w1(1)
-        load_state(2)
-        load_scales(w2_planes, w2_scales, W2_ROW)
+        load_state(2, whole)
+        load_scales(w2_scale_sb, w2_scales, W2_SCALE_ROW)
         load_w2(0)
-        load_state(3)
+        load_state(3, whole)
         load_w2(1)
-        for kind, i in ORDER:
-            {"z": load_state, "w": load_w3, "t": load_target}[kind](i)
+        load_state(4, whole)
+        load_target(range(0, 1))
+        load_w3(0)
+        load_state(5, whole)
+        load_target(range(1, 2))
+        load_w3(1)
+        load_state(6, whole)
+        load_w3(2)
+        load_state(7, whole)
+        for t in range(2, TILES, 2):
+            load_target(range(t, t + 2))
 
-        z_sorted, z_grouped, z_codes, z_scales = {}, {}, {}, {}
+        z_pairs, z_grouped, z_codes, z_scales = {}, {}, {}, {}
         w3_grouped, w3_codes, w3_scales = {}, {}, {}
         sums, acc = {}, {}
         opened = []
 
-        groups = ((0, 2), (2, 1))
-
-        def interpolate(t, group, u):
-            first, count = groups[group]
-            cols = slice(P * PACK * first, P * PACK * (first + count))
-            z_sorted[t, group, u] = ring.tile([P, count * P * 2], BF16, name="z_sorted%d_%d" % (group, u))
+        def interpolate(t, passes, u):
+            noise_sb, delta_sb = state_sb[t, passes.start]
+            pairs = ring.tile([P, 2 * P * len(passes)], BF16, name="z_pairs%d_%d" % (len(passes), u))
             nc.vector.scalar_tensor_tensor(
-                out=z_sorted[t, group, u][:].rearrange("p (q e) -> p q e", e=2),
-                in0=delta_sb[t][:, cols].rearrange("p (q u e) -> p u q e", u=2, e=2)[:, u],
+                out=pairs[:].rearrange("p (q e) -> p q e", e=2),
+                in0=delta_sb[:].rearrange("p (q u e) -> p u q e", u=2, e=2)[:, u],
                 scalar=tau_sb[:, t : t + 1],
-                in1=noise_sb[t][:, cols].rearrange("p (q u e) -> p u q e", u=2, e=2)[:, u],
+                in1=noise_sb[:].rearrange("p (q u e) -> p u q e", u=2, e=2)[:, u],
                 op0=ALU.mult,
                 op1=ALU.add,
             )
+            for g in passes:
+                first = P * (g - passes.start)
+                z_pairs[t, g, u] = pairs[:].bitcast(F32)[:, first : first + P]
 
         def interpolate_tile(t):
-            for group in range(2):
-                for u in range(2):
-                    interpolate(t, group, u)
-
-        def turn(t, group):
-            first, count = groups[group]
-            bank = psum.tile([P, 2, count, P], F32, name="turn%d" % group)
             for u in range(2):
-                words = z_sorted[t, group, u][:].bitcast(F32)
-                for i in range(count):
-                    nc.tensor.transpose(bank[:, u, i, :], words[:, P * i : P * (i + 1)], ident[:])
-            z_grouped[t, group] = ring.tile(
-                [P, count * P * PACK], BF16, name="z_grouped%d" % group, align_bytes=64
-            )
-            nc.scalar.copy(
-                out=z_grouped[t, group][:].bitcast(F32).rearrange("p (c u) -> p c u", u=2),
-                in_=bank[:].rearrange("p u i m -> p (i m) u"),
-            )
+                interpolate(t, whole, u)
 
-        def turn_tile(t):
-            turn(t, 0)
-            turn(t, 1)
+        def turn(t):
+            for passes in GROUPS:
+                bank = psum.tile([P, 2, len(passes), P], F32, name="turn%d" % passes.start)
+                for u in range(2):
+                    for g in passes:
+                        nc.tensor.transpose(bank[:, u, g - passes.start, :], z_pairs[t, g, u], identity[:])
+                grouped = ring.tile([P, K_PASS * len(passes)], BF16, name="z_grouped%d" % passes.start, align_bytes=64)
+                nc.scalar.copy(
+                    out=grouped[:].bitcast(F32).rearrange("p (c u) -> p c u", u=2),
+                    in_=bank[:].rearrange("p u g m -> p (g m) u"),
+                )
+                z_grouped[t, passes.start] = grouped
 
-        def quantize_state(t, group):
-            first, count = groups[group]
-            codes = keep.tile([P, count * P], U32, name="z_codes%d_%d" % (t, group), align_bytes=64)
-            scales = keep.tile([P, count * P], U8, name="z_scales%d_%d" % (t, group), align_bytes=64)
-            nc.vector.quantize_mx(out=codes[:].bitcast(FP8X4), scales=scales[:], in_=z_grouped[t, group][:])
-            for i in range(count):
-                z_codes[t, first + i] = codes[:, P * i : P * (i + 1)]
-                z_scales[t, first + i] = scales[:, P * i : P * (i + 1)]
+        def quantize_state(t, passes):
+            codes = keep.tile([P, P * len(passes)], U32, name="z_codes%d_%d" % (t, passes.start), align_bytes=64)
+            scales = keep.tile([P, P * len(passes)], U8, name="z_scales%d_%d" % (t, passes.start), align_bytes=64)
+            nc.vector.quantize_mx(out=codes[:].bitcast(FP8X4), scales=scales[:], in_=z_grouped[t, passes.start][:])
+            for g in passes:
+                first = P * (g - passes.start)
+                z_codes[t, g] = codes[:, first : first + P]
+                z_scales[t, g] = scales[:, first : first + P]
 
         def quantize_tile(t):
-            quantize_state(t, 0)
-            quantize_state(t, 1)
+            for passes in GROUPS:
+                quantize_state(t, passes)
 
-        def product(kind, t, h):
-            bank = psum.tile([P, HALF], F32, name="mx%d" % (len(opened) % MX_BANKS))
-            opened.append(kind)
-            sums[kind, t, h] = bank
+        def product(weight, t, h, part=slice(0, HALF)):
+            bank = psum.tile([P, part.stop - part.start], F32, name="mx%d" % (len(opened) % MX_BANKS))
+            opened.append(bank)
+            sums[weight, t, h] = bank
             cols = slice(HALF * h, HALF * (h + 1))
             for g in range(PASSES):
-                if kind == 1:
-                    rhs, rhs_scale = w1_sb[h][:, g, :].bitcast(FP4X4), w1_planes[:, g, cols]
-                elif kind == 2:
-                    rhs, rhs_scale = w2_sb[h][:, g, :].bitcast(FP8X4), w2_planes[W2_ROW:P, g, cols]
+                if weight == 1:
+                    codes, scales = w1_sb[h][:, g, :].bitcast(FP4X4), w1_scale_sb[:, g, cols]
+                elif weight == 2:
+                    codes, scales = w2_sb[h][:, g, :].bitcast(FP8X4), w2_scale_sb[W2_SCALE_ROW:P, g, cols]
                 else:
-                    rhs, rhs_scale = w3_codes[g, h][:].bitcast(FP8X4), w3_scales[g, h][:]
+                    codes, scales = w3_codes[g, h][:].bitcast(FP8X4), w3_scales[g, h][:]
                 nc.tensor.matmul_mx(
                     out=bank[:],
                     lhsT=z_codes[t, g].bitcast(FP8X4),
                     lhsT_scale=z_scales[t, g],
-                    rhs=rhs,
-                    rhs_scale=rhs_scale,
+                    rhs=codes[:, part],
+                    rhs_scale=scales[:, part],
                     start=(g == 0),
                     stop=(g == PASSES - 1),
                 )
 
         def gate(t, h):
             acc[t, h] = keep.tile([P, HALF], F32, name="acc%d_%d" % (t, h))
-            nc.scalar.activation(out=acc[t, h][:], in_=sums[1, t, h][:], func=ACT.Tanh, bias=no_bias[:])
+            nc.scalar.activation(out=acc[t, h][:], in_=sums[1, t, h][:], func=ACT.Tanh, bias=zero_bias[:])
 
         def apply_gate(t, h):
             nc.vector.tensor_tensor(out=acc[t, h][:], in0=sums[2, t, h][:], in1=acc[t, h][:], op=ALU.mult)
 
-        def subtract_target(t, h):
-            engine = nc.vector if h == 1 and t >= TILES - V_TAIL else nc.gpsimd
+        def subtract_target(engine, t, h, result):
             engine.tensor_tensor(
-                out=acc[t, h][:],
-                in0=acc[t, h][:],
-                in1=target_sb[t // 2][:, t % 2, HALF * h : HALF * (h + 1)],
-                op=ALU.subtract,
+                out=result[:], in0=acc[t, h][:], in1=target_sb[t][:, HALF * h : HALF * (h + 1)], op=ALU.subtract
             )
+            acc[t, h] = result
 
-        def finish(t, h):
-            nc.vector.tensor_tensor(out=acc[t, h][:], in0=sums[3, t, h][:], in1=acc[t, h][:], op=ALU.add)
-            nc.sync.dma_start(out=out_t[t][:, HALF * h : HALF * (h + 1)], in_=acc[t, h][:])
+        def finish(t, h, part=slice(0, HALF)):
+            nc.vector.tensor_tensor(out=acc[t, h][:, part], in0=sums[3, t, h][:], in1=acc[t, h][:, part], op=ALU.add)
+            cols = slice(HALF * h + part.start, HALF * h + part.stop)
+            nc.sync.dma_start(out=out_t[t][:, cols], in_=acc[t, h][:, part])
 
-        per_block = HALF // PIECE
-        to_group = [(g, h, i) for h in range(HALVES) for g in range(PASSES) for i in range(per_block)]
+        to_group = [(g, h, c) for h in range(HALVES) for g in range(PASSES) for c in range(0, HALF, PIECE)]
         to_quantize = []
 
-        def group_w3():
-            g, h, i = to_group.pop(0)
-            if i == 0:
-                w3_grouped[g, h] = ring.tile([P, HALF, PACK], BF16, name="w3_grouped", align_bytes=64)
-            c0 = HALF * h + PIECE * i
-            nc.scalar.copy(
-                out=w3_grouped[g, h][:, PIECE * i : PIECE * (i + 1), :].rearrange("p (c i) j -> p c j i", i=4),
-                in_=w3_sb[g][:, :, c0 : c0 + PIECE].rearrange("p j (c i) -> p c j i", i=4),
-            )
-            if i == per_block - 1:
-                to_quantize.append((g, h))
+        def group_w3(pieces):
+            for g, h, c in to_group[:pieces]:
+                if c == 0:
+                    w3_grouped[g, h] = ring.tile([P, HALF, PACK], BF16, name="w3_grouped", align_bytes=64)
+                cols = slice(HALF * h + c, HALF * h + c + PIECE)
+                nc.scalar.copy(
+                    out=w3_grouped[g, h][:, c : c + PIECE, :].rearrange("p (c i) j -> p c j i", i=4),
+                    in_=w3_sb[g][:, :, cols].rearrange("p j (c i) -> p c j i", i=4),
+                )
+                to_group.remove((g, h, c))
+                if c + PIECE == HALF:
+                    to_quantize.append((g, h))
 
         def quantize_w3():
-            for g, h in list(to_quantize):
+            for g, h in to_quantize:
                 w3_codes[g, h] = keep.tile([P, HALF], U32, name="w3_codes%d_%d" % (g, h), align_bytes=64)
                 w3_scales[g, h] = keep.tile([P, HALF], U8, name="w3_scales%d_%d" % (g, h), align_bytes=64)
                 nc.vector.quantize_mx(
@@ -232,83 +241,69 @@ def tile_straight_path_regression_error_s10_kernel(
                 )
             to_quantize.clear()
 
-        interpolate_tile(0)
-        turn_tile(0)
-        interpolate(1, 0, 0)
-        quantize_state(0, 0)
-        interpolate(1, 0, 1)
-        quantize_state(0, 1)
-        interpolate(1, 1, 0)
-        interpolate(1, 1, 1)
+        for passes in GROUPS:
+            for u in range(2):
+                interpolate(0, passes, u)
+        turn(0)
+        for u in range(2):
+            interpolate(1, GROUPS[0], u)
+            quantize_state(0, GROUPS[u])
+        for u in range(2):
+            interpolate(1, GROUPS[1], u)
         product(1, 0, 0)
-        turn_tile(1)
+        turn(1)
         product(1, 0, 1)
         quantize_tile(1)
+        interpolate_tile(2)
         gate(0, 0)
         gate(0, 1)
-        interpolate_tile(2)
         product(1, 1, 0)
         product(1, 1, 1)
         gate(1, 0)
-        turn_tile(2)
-        gate(1, 1)
-        product(2, 0, 0)
-        product(2, 1, 0)
-        quantize_tile(2)
-        apply_gate(0, 0)
-        interpolate_tile(3)
-        apply_gate(1, 0)
-        product(1, 2, 0)
-        product(1, 2, 1)
-        gate(2, 0)
-        turn_tile(3)
-        gate(2, 1)
-        product(2, 2, 0)
-        product(2, 0, 1)
-        product(2, 1, 1)
-        quantize_tile(3)
-        interpolate_tile(4)
-        apply_gate(2, 0)
-        apply_gate(0, 1)
 
-        late = (1, 1)
-        for s in range(3, TILES + 1):
+        gated = [(t, h) for h in range(HALVES) for t in range(EARLY_TILES)]
+        gated = gated + [(t, h) for t in range(EARLY_TILES, TILES) for h in range(HALVES)]
+        early_units = [(t, h) for t in range(2) for h in range(HALVES)]
+        first_early_step = TILES - 1 - len(early_units)
+        vector_units = [(2 + i, 0) for i in range(VECTOR_UNITS)]
+        for s in range(2, TILES + 2):
+            pair = gated[2 * (s - 2) : 2 * (s - 1)]
+            if s <= TILES:
+                gate(s - 1, 1)
+            if s < TILES:
+                turn(s)
+            for t, h in pair:
+                product(2, t, h)
+            if s < TILES:
+                quantize_tile(s)
+            if s >= FIRST_W3_STEP:
+                group_w3(PIECES_PER_STEP)
             if s + 1 < TILES:
-                turn_tile(s + 1)
+                interpolate_tile(s + 1)
+            if s + 1 == TILES:
+                for t, h in vector_units:
+                    subtract_target(nc.vector, t, h, acc[t, h])
+            quantize_w3()
+            if first_early_step <= s < TILES - 1:
+                t, h = early_units[s - first_early_step]
+                freed = keep.tile([P, HALF], F32, name="noise%d_0" % (s + 1))
+                subtract_target(nc.gpsimd, t, h, freed)
             if s < TILES:
                 product(1, s, 0)
                 product(1, s, 1)
-            apply_gate(*late)
-            if s + 1 < TILES:
-                quantize_tile(s + 1)
-            if s < TILES:
                 gate(s, 0)
-                gate(s, 1)
-            if s + 2 < TILES:
-                interpolate_tile(s + 2)
-            quantize_w3()
-            if s > 3:
-                product(2, s - 1, 0)
-            product(2, s - 1, 1)
-            if s >= FIRST_W3_STEP:
-                for i in range(PIECES_PER_STEP):
-                    group_w3()
-            if s > 3:
-                apply_gate(s - 1, 0)
-            late = (s - 1, 1)
-        apply_gate(*late)
-        while (PASSES - 1, 0) not in w3_grouped or to_group[0][1] == 0:
-            group_w3()
-        quantize_w3()
+            for t, h in pair:
+                apply_gate(t, h)
 
-        for t in range(TILES):
-            subtract_target(t, 0)
+        rest = [(t, h) for t in range(2, TILES) for h in range(HALVES) if (t, h) not in vector_units]
+        for t, h in sorted(rest, key=lambda unit: (unit[0] + SECOND_HALF_LAG * unit[1], unit[1])):
+            subtract_target(nc.gpsimd, t, h, acc[t, h])
+
         for h in range(HALVES):
             for t in range(TILES):
-                product(3, t, h)
-                if h == 1:
-                    subtract_target(t, h)
-                finish(t, h)
+                last = (t, h) == (TILES - 1, HALVES - 1)
+                for part in (slice(0, HALF // 2), slice(HALF // 2, HALF)) if last else (slice(0, HALF),):
+                    product(3, t, h, part)
+                    finish(t, h, part)
                 quantize_w3()
-                for i in range(min(2, len(to_group))):
-                    group_w3()
+                group_w3(2)

@@ -29,7 +29,8 @@ W2_SCALE_ROW = 4
 EARLY_TILES = 3
 PIECE = 128
 PIECES_PER_STEP = 3
-FIRST_W3_STEP = 4
+FIRST_W3_STEP = 3
+AHEAD_STEP = 3
 VECTOR_UNITS = 3
 SECOND_HALF_LAG = 3
 
@@ -61,7 +62,8 @@ def tile_straight_path_regression_error_s10_kernel(
         make_identity(nc, identity[:])
 
         tau_sb = keep.tile([P, TILES], BF16, name="tau_sb")
-        state_sb, w1_sb, w2_sb, w3_sb, target_sb = {}, {}, {}, {}, {}
+        w1_sb = keep.tile([P, PASSES, 2 * N], U8, name="w1_sb", align_bytes=64)
+        state_sb, w2_sb, w3_sb, target_sb = {}, {}, {}, {}
 
         def load_state(t, passes):
             cols = slice(K_PASS * passes.start, K_PASS * passes.stop)
@@ -76,11 +78,6 @@ def tile_straight_path_regression_error_s10_kernel(
             rows = scales.rearrange("g (Q r) n -> r Q g n", r=4)
             for r in range(4):
                 nc.sync.dma_start(out=scale_sb[first_row + r : P : 32, :, :].bitcast(I32), in_=rows[r].bitcast(I32))
-
-        def load_w1(h):
-            w1_sb[h] = keep.tile([P, PASSES, 2 * HALF], U8, name="w1_%d" % h, align_bytes=64)
-            words = w1_words.rearrange("g p b -> p g b")[:, :, 2 * HALF * h : 2 * HALF * (h + 1)]
-            nc.sync.dma_start(out=w1_sb[h][:].bitcast(I32), in_=words.bitcast(I32))
 
         def load_w2(h):
             w2_sb[h] = keep.tile([P, PASSES, HALF], U32, name="w2_%d" % h, align_bytes=64)
@@ -100,27 +97,24 @@ def tile_straight_path_regression_error_s10_kernel(
 
         whole = range(PASSES)
         nc.sync.dma_start(out=tau_sb[:], in_=tau.rearrange("(p t) o -> p (t o)", t=TILES))
-        load_state(0, GROUPS[0])
-        load_state(0, GROUPS[1])
-        load_state(1, GROUPS[0])
+        for passes in GROUPS:
+            load_state(0, passes)
+        load_state(1, whole)
         load_scales(w1_scale_sb, w1_scales, 0)
-        load_w1(0)
-        load_state(1, GROUPS[1])
-        load_w1(1)
+        nc.sync.dma_start(out=w1_sb[:].bitcast(I32), in_=w1_words.rearrange("g p b -> p g b").bitcast(I32))
         load_state(2, whole)
         load_scales(w2_scale_sb, w2_scales, W2_SCALE_ROW)
         load_w2(0)
         load_state(3, whole)
         load_w2(1)
         load_state(4, whole)
-        load_target(range(0, 1))
         load_w3(0)
         load_state(5, whole)
-        load_target(range(1, 2))
-        load_w3(1)
+        load_target(range(0, 2))
         load_state(6, whole)
-        load_w3(2)
+        load_w3(1)
         load_state(7, whole)
+        load_w3(2)
         for t in range(2, TILES, 2):
             load_target(range(t, t + 2))
 
@@ -154,7 +148,8 @@ def tile_straight_path_regression_error_s10_kernel(
                 for u in range(2):
                     for g in passes:
                         nc.tensor.transpose(bank[:, u, g - passes.start, :], z_pairs[t, g, u], identity[:])
-                grouped = ring.tile([P, K_PASS * len(passes)], BF16, name="z_grouped%d" % passes.start, align_bytes=64)
+                name = "z_grouped%d_%d" % (t, passes.start)
+                grouped = keep.tile([P, K_PASS * len(passes)], BF16, name=name, align_bytes=64)
                 nc.scalar.copy(
                     out=grouped[:].bitcast(F32).rearrange("p (c u) -> p c u", u=2),
                     in_=bank[:].rearrange("p u g m -> p (g m) u"),
@@ -181,7 +176,7 @@ def tile_straight_path_regression_error_s10_kernel(
             cols = slice(HALF * h, HALF * (h + 1))
             for g in range(PASSES):
                 if weight == 1:
-                    codes, scales = w1_sb[h][:, g, :].bitcast(FP4X4), w1_scale_sb[:, g, cols]
+                    codes, scales = w1_sb[:, g, 2 * cols.start : 2 * cols.stop].bitcast(FP4X4), w1_scale_sb[:, g, cols]
                 elif weight == 2:
                     codes, scales = w2_sb[h][:, g, :].bitcast(FP8X4), w2_scale_sb[W2_SCALE_ROW:P, g, cols]
                 else:
@@ -214,7 +209,8 @@ def tile_straight_path_regression_error_s10_kernel(
             cols = slice(HALF * h + part.start, HALF * h + part.stop)
             nc.sync.dma_start(out=out_t[t][:, cols], in_=acc[t, h][:, part])
 
-        to_group = [(g, h, c) for h in range(HALVES) for g in range(PASSES) for c in range(0, HALF, PIECE)]
+        blocks = [(0, h) for h in range(HALVES)] + [(g, h) for h in range(HALVES) for g in range(1, PASSES)]
+        to_group = [(g, h, c) for g, h in blocks for c in range(0, HALF, PIECE)]
         to_quantize = []
 
         def group_w3(pieces):
@@ -245,13 +241,10 @@ def tile_straight_path_regression_error_s10_kernel(
             for u in range(2):
                 interpolate(0, passes, u)
         turn(0)
-        for u in range(2):
-            interpolate(1, GROUPS[0], u)
-            quantize_state(0, GROUPS[u])
-        for u in range(2):
-            interpolate(1, GROUPS[1], u)
-        product(1, 0, 0)
+        interpolate_tile(1)
+        quantize_tile(0)
         turn(1)
+        product(1, 0, 0)
         product(1, 0, 1)
         quantize_tile(1)
         interpolate_tile(2)
@@ -264,36 +257,46 @@ def tile_straight_path_regression_error_s10_kernel(
         gated = [(t, h) for h in range(HALVES) for t in range(EARLY_TILES)]
         gated = gated + [(t, h) for t in range(EARLY_TILES, TILES) for h in range(HALVES)]
         early_units = [(t, h) for t in range(2) for h in range(HALVES)]
-        first_early_step = TILES - 1 - len(early_units)
+        first_early_step = TILES - len(early_units)
         vector_units = [(2 + i, 0) for i in range(VECTOR_UNITS)]
         for s in range(2, TILES + 2):
-            pair = gated[2 * (s - 2) : 2 * (s - 1)]
-            if s <= TILES:
+            now = gated[: 3 if s == AHEAD_STEP else 2]
+            gated = gated[len(now) :]
+            if s <= AHEAD_STEP:
                 gate(s - 1, 1)
             if s < TILES:
                 turn(s)
-            for t, h in pair:
+            if AHEAD_STEP < s <= TILES:
+                gate(s - 1, 0)
+            for t, h in now:
                 product(2, t, h)
+            if AHEAD_STEP <= s < TILES - 1:
+                interpolate_tile(s + 1)
+            quantize_w3()
             if s < TILES:
                 quantize_tile(s)
-            if s >= FIRST_W3_STEP:
-                group_w3(PIECES_PER_STEP)
-            if s + 1 < TILES:
+            if s < AHEAD_STEP:
                 interpolate_tile(s + 1)
-            if s + 1 == TILES:
+            if s >= FIRST_W3_STEP:
+                group_w3(PIECES_PER_STEP + (s == AHEAD_STEP))
+            if s == TILES - 1:
                 for t, h in vector_units:
                     subtract_target(nc.vector, t, h, acc[t, h])
-            quantize_w3()
-            if first_early_step <= s < TILES - 1:
+            if first_early_step <= s < TILES:
                 t, h = early_units[s - first_early_step]
-                freed = keep.tile([P, HALF], F32, name="noise%d_0" % (s + 1))
+                freed = keep.tile([P, HALF], F32, name="z_grouped%d_0" % s, align_bytes=64)
                 subtract_target(nc.gpsimd, t, h, freed)
+            if AHEAD_STEP < s <= TILES:
+                product(1, s - 1, 1)
+                gate(s - 1, 1)
             if s < TILES:
                 product(1, s, 0)
+            if s < AHEAD_STEP:
                 product(1, s, 1)
                 gate(s, 0)
-            for t, h in pair:
+            for t, h in now:
                 apply_gate(t, h)
+        quantize_w3()
 
         rest = [(t, h) for t in range(2, TILES) for h in range(HALVES) if (t, h) not in vector_units]
         for t, h in sorted(rest, key=lambda unit: (unit[0] + SECOND_HALF_LAG * unit[1], unit[1])):

@@ -77,7 +77,7 @@ def tile_straight_path_regression_error_s10_kernel(
         def load_scales(scale_sb, scales, first_row):
             rows = scales.rearrange("g (Q r) n -> r Q g n", r=4)
             for r in range(4):
-                nc.sync.dma_start(out=scale_sb[first_row + r : P : 32, :, :].bitcast(I32), in_=rows[r].bitcast(I32))
+                nc.gpsimd.dma_start(out=scale_sb[first_row + r : P : 32, :, :].bitcast(I32), in_=rows[r].bitcast(I32))
 
         def load_w2(h):
             w2_sb[h] = keep.tile([P, PASSES, HALF], U32, name="w2_%d" % h, align_bytes=64)
@@ -95,15 +95,16 @@ def tile_straight_path_regression_error_s10_kernel(
             for t in tiles:
                 target_sb[t] = rows[:, t - tiles.start, :]
 
+        load_scales(w1_scale_sb, w1_scales, 0)
+        load_scales(w2_scale_sb, w2_scales, W2_SCALE_ROW)
+
         whole = range(PASSES)
         nc.sync.dma_start(out=tau_sb[:], in_=tau.rearrange("(p t) o -> p (t o)", t=TILES))
-        for passes in GROUPS:
-            load_state(0, passes)
-        load_state(1, whole)
-        load_scales(w1_scale_sb, w1_scales, 0)
+        for t in range(2):
+            for passes in GROUPS:
+                load_state(t, passes)
         nc.sync.dma_start(out=w1_sb[:].bitcast(I32), in_=w1_words.rearrange("g p b -> p g b").bitcast(I32))
         load_state(2, whole)
-        load_scales(w2_scale_sb, w2_scales, W2_SCALE_ROW)
         load_w2(0)
         load_state(3, whole)
         load_w2(1)
@@ -241,7 +242,9 @@ def tile_straight_path_regression_error_s10_kernel(
             for u in range(2):
                 interpolate(0, passes, u)
         turn(0)
-        interpolate_tile(1)
+        for passes in GROUPS:
+            for u in range(2):
+                interpolate(1, passes, u)
         quantize_tile(0)
         turn(1)
         product(1, 0, 0)

from contextlib import ExitStack

import concourse.mybir as mybir
from concourse.masks import make_identity

M, D, N = 1024, 1536, 1024
FLOPS = 3 * 2 * M * D * N

F32 = mybir.dt.float32
BF16 = mybir.dt.bfloat16
I32 = mybir.dt.int32
U32 = mybir.dt.uint32
U8 = mybir.dt.uint8
FP8X4 = mybir.dt.float8_e4m3fn_x4
FP4X4 = mybir.dt.float4_e2m1fn_x4
ALU = mybir.AluOpType
ACT = mybir.ActivationFunctionType

P = 128
PACK = 4
K_PASS = P * PACK
PASSES = D // K_PASS
TILES = M // P
HALF = 512
HALVES = N // HALF
GROUPS = (range(0, 2), range(2, 3))
MX_BANKS = 6
W2_SCALE_ROW = 4
EARLY_TILES = 3
PIECE = 128
PIECES_PER_STEP = 3
FIRST_W3_STEP = 3
AHEAD_STEP = 3
VECTOR_UNITS = 3
SECOND_HALF_LAG = 3


def tile_straight_path_regression_error_s10_kernel(
    tc, noise, delta, tau, w1_words, w1_scales, w2_words, w2_scales, w3, target, out
):
    nc = tc.nc
    noise_t = noise.rearrange("(p t) k -> t p k", t=TILES)
    delta_t = delta.rearrange("(p t) k -> t p k", t=TILES)
    target_p = target.rearrange("(p t) n -> p t n", t=TILES)
    out_t = out.rearrange("(p t) n -> t p n", t=TILES)

    with ExitStack() as ctx:
        keep = ctx.enter_context(tc.tile_pool(name="keep", bufs=1))
        ring = ctx.enter_context(tc.tile_pool(name="ring", bufs=3))
        psum = ctx.enter_context(tc.psum_pool(name="psum", bufs=1))
        ctx.enter_context(tc.manual_schedule())

        w1_scale_sb = keep.tile([P, PASSES, N], U8, name="w1_scale_sb", align_bytes=64)
        w2_scale_sb = keep.tile([P, PASSES, N], U8, name="w2_scale_sb", align_bytes=64)
        nc.vector.memset(w1_scale_sb[:].bitcast(I32), 0)
        nc.vector.memset(w2_scale_sb[:].bitcast(I32), 0)
        zero = keep.tile([P, 1], F32, name="zero")
        nc.vector.memset(zero[:], 0.0)
        zero_bias = keep.tile([P, 1], F32, name="zero_bias")
        nc.scalar.activation(out=zero_bias[:], in_=zero[:], func=ACT.Tanh)
        identity = keep.tile([P, P], F32, name="identity")
        make_identity(nc, identity[:])

        tau_sb = keep.tile([P, TILES], BF16, name="tau_sb")
        w1_sb = keep.tile([P, PASSES, 2 * N], U8, name="w1_sb", align_bytes=64)
        state_sb, w2_sb, w3_sb, target_sb = {}, {}, {}, {}

        def load_state(t, passes):
            cols = slice(K_PASS * passes.start, K_PASS * passes.stop)
            width = K_PASS * len(passes)
            noise_sb = keep.tile([P, width], BF16, name="noise%d_%d" % (t, passes.start))
            delta_sb = keep.tile([P, width], BF16, name="delta%d_%d" % (t, passes.start))
            nc.sync.dma_start(out=noise_sb[:], in_=noise_t[t][:, cols])
            nc.sync.dma_start(out=delta_sb[:], in_=delta_t[t][:, cols])
            state_sb[t, passes.start] = (noise_sb, delta_sb)

        def load_scales(scale_sb, scales, first_row):
            rows = scales.rearrange("g (Q r) n -> r Q g n", r=4)
            for r in range(4):
                nc.gpsimd.dma_start(out=scale_sb[first_row + r : P : 32, :, :].bitcast(I32), in_=rows[r].bitcast(I32))

        def load_w2(h):
            w2_sb[h] = keep.tile([P, PASSES, HALF], U32, name="w2_%d" % h, align_bytes=64)
            words = w2_words.rearrange("g p n j -> p g (n j)")[:, :, PACK * HALF * h : PACK * HALF * (h + 1)]
            nc.sync.dma_start(out=w2_sb[h][:].bitcast(I32), in_=words.bitcast(I32))

        def load_w3(g):
            w3_sb[g] = keep.tile([P, PACK, N], BF16, name="w3_%d" % g)
            rows = w3[K_PASS * g : K_PASS * (g + 1), :]
            nc.sync.dma_start(out=w3_sb[g][:], in_=rows.rearrange("(p j) n -> p j n", j=PACK))

        def load_target(tiles):
            rows = keep.tile([P, len(tiles), N], BF16, name="target%d" % tiles.start)
            nc.sync.dma_start(out=rows[:], in_=target_p[:, tiles.start : tiles.stop, :])
            for t in tiles:
                target_sb[t] = rows[:, t - tiles.start, :]

        load_scales(w1_scale_sb, w1_scales, 0)
        load_scales(w2_scale_sb, w2_scales, W2_SCALE_ROW)

        whole = range(PASSES)
        nc.sync.dma_start(out=tau_sb[:], in_=tau.rearrange("(p t) o -> p (t o)", t=TILES))
        for t in range(2):
            for passes in GROUPS:
                load_state(t, passes)
        nc.sync.dma_start(out=w1_sb[:].bitcast(I32), in_=w1_words.rearrange("g p b -> p g b").bitcast(I32))
        load_state(2, whole)
        load_w2(0)
        load_state(3, whole)
        load_w2(1)
        load_state(4, whole)
        load_w3(0)
        load_state(5, whole)
        load_target(range(0, 2))
        load_state(6, whole)
        load_w3(1)
        load_state(7, whole)
        load_w3(2)
        for t in range(2, TILES, 2):
            load_target(range(t, t + 2))

        z_pairs, z_grouped, z_codes, z_scales = {}, {}, {}, {}
        w3_grouped, w3_codes, w3_scales = {}, {}, {}
        sums, acc = {}, {}
        opened = []

        def interpolate(t, passes, u):
            noise_sb, delta_sb = state_sb[t, passes.start]
            pairs = ring.tile([P, 2 * P * len(passes)], BF16, name="z_pairs%d_%d" % (len(passes), u))
            nc.vector.scalar_tensor_tensor(
                out=pairs[:].rearrange("p (q e) -> p q e", e=2),
                in0=delta_sb[:].rearrange("p (q u e) -> p u q e", u=2, e=2)[:, u],
                scalar=tau_sb[:, t : t + 1],
                in1=noise_sb[:].rearrange("p (q u e) -> p u q e", u=2, e=2)[:, u],
                op0=ALU.mult,
                op1=ALU.add,
            )
            for g in passes:
                first = P * (g - passes.start)
                z_pairs[t, g, u] = pairs[:].bitcast(F32)[:, first : first + P]

        def interpolate_tile(t):
            for u in range(2):
                interpolate(t, whole, u)

        def turn(t):
            for passes in GROUPS:
                bank = psum.tile([P, 2, len(passes), P], F32, name="turn%d" % passes.start)
                for u in range(2):
                    for g in passes:
                        nc.tensor.transpose(bank[:, u, g - passes.start, :], z_pairs[t, g, u], identity[:])
                name = "z_grouped%d_%d" % (t, passes.start)
                grouped = keep.tile([P, K_PASS * len(passes)], BF16, name=name, align_bytes=64)
                nc.scalar.copy(
                    out=grouped[:].bitcast(F32).rearrange("p (c u) -> p c u", u=2),
                    in_=bank[:].rearrange("p u g m -> p (g m) u"),
                )
                z_grouped[t, passes.start] = grouped

        def quantize_state(t, passes):
            codes = keep.tile([P, P * len(passes)], U32, name="z_codes%d_%d" % (t, passes.start), align_bytes=64)
            scales = keep.tile([P, P * len(passes)], U8, name="z_scales%d_%d" % (t, passes.start), align_bytes=64)
            nc.vector.quantize_mx(out=codes[:].bitcast(FP8X4), scales=scales[:], in_=z_grouped[t, passes.start][:])
            for g in passes:
                first = P * (g - passes.start)
                z_codes[t, g] = codes[:, first : first + P]
                z_scales[t, g] = scales[:, first : first + P]

        def quantize_tile(t):
            for passes in GROUPS:
                quantize_state(t, passes)

        def product(weight, t, h, part=slice(0, HALF)):
            bank = psum.tile([P, part.stop - part.start], F32, name="mx%d" % (len(opened) % MX_BANKS))
            opened.append(bank)
            sums[weight, t, h] = bank
            cols = slice(HALF * h, HALF * (h + 1))
            for g in range(PASSES):
                if weight == 1:
                    codes, scales = w1_sb[:, g, 2 * cols.start : 2 * cols.stop].bitcast(FP4X4), w1_scale_sb[:, g, cols]
                elif weight == 2:
                    codes, scales = w2_sb[h][:, g, :].bitcast(FP8X4), w2_scale_sb[W2_SCALE_ROW:P, g, cols]
                else:
                    codes, scales = w3_codes[g, h][:].bitcast(FP8X4), w3_scales[g, h][:]
                nc.tensor.matmul_mx(
                    out=bank[:],
                    lhsT=z_codes[t, g].bitcast(FP8X4),
                    lhsT_scale=z_scales[t, g],
                    rhs=codes[:, part],
                    rhs_scale=scales[:, part],
                    start=(g == 0),
                    stop=(g == PASSES - 1),
                )

        def gate(t, h):
            acc[t, h] = keep.tile([P, HALF], F32, name="acc%d_%d" % (t, h))
            nc.scalar.activation(out=acc[t, h][:], in_=sums[1, t, h][:], func=ACT.Tanh, bias=zero_bias[:])

        def apply_gate(t, h):
            nc.vector.tensor_tensor(out=acc[t, h][:], in0=sums[2, t, h][:], in1=acc[t, h][:], op=ALU.mult)

        def subtract_target(engine, t, h, result):
            engine.tensor_tensor(
                out=result[:], in0=acc[t, h][:], in1=target_sb[t][:, HALF * h : HALF * (h + 1)], op=ALU.subtract
            )
            acc[t, h] = result

        def finish(t, h, part=slice(0, HALF)):
            nc.vector.tensor_tensor(out=acc[t, h][:, part], in0=sums[3, t, h][:], in1=acc[t, h][:, part], op=ALU.add)
            cols = slice(HALF * h + part.start, HALF * h + part.stop)
            nc.sync.dma_start(out=out_t[t][:, cols], in_=acc[t, h][:, part])

        blocks = [(0, h) for h in range(HALVES)] + [(g, h) for h in range(HALVES) for g in range(1, PASSES)]
        to_group = [(g, h, c) for g, h in blocks for c in range(0, HALF, PIECE)]
        to_quantize = []

        def group_w3(pieces):
            for g, h, c in to_group[:pieces]:
                if c == 0:
                    w3_grouped[g, h] = ring.tile([P, HALF, PACK], BF16, name="w3_grouped", align_bytes=64)
                cols = slice(HALF * h + c, HALF * h + c + PIECE)
                nc.scalar.copy(
                    out=w3_grouped[g, h][:, c : c + PIECE, :].rearrange("p (c i) j -> p c j i", i=4),
                    in_=w3_sb[g][:, :, cols].rearrange("p j (c i) -> p c j i", i=4),
                )
                to_group.remove((g, h, c))
                if c + PIECE == HALF:
                    to_quantize.append((g, h))

        def quantize_w3():
            for g, h in to_quantize:
                w3_codes[g, h] = keep.tile([P, HALF], U32, name="w3_codes%d_%d" % (g, h), align_bytes=64)
                w3_scales[g, h] = keep.tile([P, HALF], U8, name="w3_scales%d_%d" % (g, h), align_bytes=64)
                nc.vector.quantize_mx(
                    out=w3_codes[g, h][:].bitcast(FP8X4),
                    scales=w3_scales[g, h][:],
                    in_=w3_grouped[g, h][:].rearrange("p c j -> p (c j)"),
                )
            to_quantize.clear()

        for passes in GROUPS:
            for u in range(2):
                interpolate(0, passes, u)
        turn(0)
        for passes in GROUPS:
            for u in range(2):
                interpolate(1, passes, u)
        quantize_tile(0)
        turn(1)
        product(1, 0, 0)
        product(1, 0, 1)
        quantize_tile(1)
        interpolate_tile(2)
        gate(0, 0)
        gate(0, 1)
        product(1, 1, 0)
        product(1, 1, 1)
        gate(1, 0)

        gated = [(t, h) for h in range(HALVES) for t in range(EARLY_TILES)]
        gated = gated + [(t, h) for t in range(EARLY_TILES, TILES) for h in range(HALVES)]
        early_units = [(t, h) for t in range(2) for h in range(HALVES)]
        first_early_step = TILES - len(early_units)
        vector_units = [(2 + i, 0) for i in range(VECTOR_UNITS)]
        for s in range(2, TILES + 2):
            now = gated[: 3 if s == AHEAD_STEP else 2]
            gated = gated[len(now) :]
            if s <= AHEAD_STEP:
                gate(s - 1, 1)
            if s < TILES:
                turn(s)
            if AHEAD_STEP < s <= TILES:
                gate(s - 1, 0)
            for t, h in now:
                product(2, t, h)
            if AHEAD_STEP <= s < TILES - 1:
                interpolate_tile(s + 1)
            quantize_w3()
            if s < TILES:
                quantize_tile(s)
            if s < AHEAD_STEP:
                interpolate_tile(s + 1)
            if s >= FIRST_W3_STEP:
                group_w3(PIECES_PER_STEP + (s == AHEAD_STEP))
            if s == TILES - 1:
                for t, h in vector_units:
                    subtract_target(nc.vector, t, h, acc[t, h])
            if first_early_step <= s < TILES:
                t, h = early_units[s - first_early_step]
                freed = keep.tile([P, HALF], F32, name="z_grouped%d_0" % s, align_bytes=64)
                subtract_target(nc.gpsimd, t, h, freed)
            if AHEAD_STEP < s <= TILES:
                product(1, s - 1, 1)
                gate(s - 1, 1)
            if s < TILES:
                product(1, s, 0)
            if s < AHEAD_STEP:
                product(1, s, 1)
                gate(s, 0)
            for t, h in now:
                apply_gate(t, h)
        quantize_w3()

        rest = [(t, h) for t in range(2, TILES) for h in range(HALVES) if (t, h) not in vector_units]
        for t, h in sorted(rest, key=lambda unit: (unit[0] + SECOND_HALF_LAG * unit[1], unit[1])):
            subtract_target(nc.gpsimd, t, h, acc[t, h])

        for h in range(HALVES):
            for t in range(TILES):
                last = (t, h) == (TILES - 1, HALVES - 1)
                for part in (slice(0, HALF // 2), slice(HALF // 2, HALF)) if last else (slice(0, HALF),):
                    product(3, t, h, part)
                    finish(t, h, part)
                quantize_w3()
                group_w3(2)
